import numpy as np
import ml_dtypes


def mxq(x, axis, fmt="e4m3"):
    dtype, down = {"e4m3": (ml_dtypes.float8_e4m3fn, 7), "e5m2": (ml_dtypes.float8_e5m2, 14)}[fmt]
    v = np.moveaxis(np.asarray(x, np.float32).astype(ml_dtypes.bfloat16).astype(np.float64), axis, -1)
    blocks = v.reshape(v.shape[:-1] + (-1, 32))
    amax = np.abs(blocks).max(-1, keepdims=True)
    byte = np.maximum(np.where(amax > 0, np.frexp(amax)[1] - 1 + 127, 0) - down, 1)
    scale = np.exp2(byte - 127.0)
    codes = (blocks / scale).astype(np.float32).astype(dtype).astype(np.float64)
    return np.moveaxis((codes * scale).reshape(v.shape), -1, axis)


WIDE = False


def mx_kscale(k):
    if not WIDE:
        return np.ones(k)
    levels = np.array([10, -10, 5, -5, 0])
    if k % 512:
        return np.exp2(np.random.permutation(np.resize(levels, k // 32))).repeat(32)
    a = np.empty((k // 512, 16))
    for p in range(k // 512):
        a[p, :8] = np.random.permutation(np.resize(levels, 8))
        for g in range(8):
            far = levels[np.abs(levels - a[p, g]) >= 10]
            a[p, g + 8] = far[np.random.randint(len(far))]
    return np.exp2(a.ravel()).repeat(32)


def f64(x):
    return np.asarray(x).astype(np.float64)


def striped(idx):
    return np.tile(idx.reshape(-1, 16).T, (8, 1)).astype(np.uint16)


def unstriped(offs):
    return offs[:16].T.reshape(-1).astype(np.int64)


def striped8(idx):
    return np.concatenate([x.reshape(-1, 16).T for x in idx]).astype(np.uint16)


def runs(offs, k):
    lists = np.stack([offs[16 * r : 16 * r + 16].T.reshape(-1) for r in range(8)]).astype(np.int64)
    return lists[np.arange(k) % 512 // 64]


def pack_weight(w):
    k, n = w.shape
    w = f64(np.asarray(w, np.float32).astype(ml_dtypes.bfloat16)).reshape(k // 32, 32, n)
    amax = np.abs(w).max(1)
    byte = np.clip(np.where(amax > 0, np.frexp(amax)[1] - 1 + 127 - 7, 1), 1, 254)
    scaled = (w * np.exp2(127.0 - byte)[:, None, :]).reshape(k, n).astype(np.float32)
    words = np.ascontiguousarray(scaled.reshape(k // 512, 128, 4, n).transpose(0, 1, 3, 2)).astype(ml_dtypes.float8_e4m3fn).view(np.uint8)
    return words, np.ascontiguousarray(byte.astype(np.uint8).reshape(k // 512, 16, n))


def unpack_weight(words, scales):
    g, p, n, _ = words.shape
    vals = np.ascontiguousarray(words).view(ml_dtypes.float8_e4m3fn).astype(np.float64) * np.repeat(np.exp2(scales.astype(np.float64) - 127.0), 8, axis=1)[..., None]
    return vals.transpose(0, 1, 3, 2).reshape(g * 512, n)


def sigmoid(v):
    return 1.0 / (1.0 + np.exp(-np.maximum(v, -700.0)))


K, T, S, V, N, G, H, W = 512, 2048, 512, 256, 512, 2048, 512, 1024


def setup_inputs():
    n = np.random.standard_normal
    s = mx_kscale(K)[:, None]
    u = mx_kscale(S)
    packed_xT = pack_weight(n((K, T)) * s)
    packed_dT = pack_weight(n((K, G)) / s)
    return {
        "x_words": packed_xT[0],
        "x_scales": packed_xT[1],
        "d_words": packed_dT[0],
        "d_scales": packed_dT[1],
        "gn": (np.random.uniform(0.5, 1.5, (H, 1)) * u[:, None]).astype(np.float32),
        "w1": (n((H, N)) / np.sqrt(H) / u[:, None]).astype(np.float32),
        "offs": striped(np.random.permutation(T)[:S]),
        "k1": striped8(np.random.randint(0, G, (8, H))),
        "n1": striped(np.random.permutation(S)),
        "n2": striped(np.random.randint(0, V, W)),
    }


def reference(x_words, x_scales, d_words, d_scales, gn, w1, offs, k1, n1, n2):
    d_k1 = unpack_weight(d_words, d_scales)[np.arange(K)[:, None], runs(k1, K)]
    xq = unpack_weight(x_words, x_scales)[:, unstriped(offs)]
    h = 0.0625 * (d_k1.T @ xq)
    ln = h[:, unstriped(n1)]
    mx = ln.reshape(H, V, 2).max(axis=2)
    mn = ln.reshape(H, V, 2).min(axis=2)
    z = f64(gn) * (mx * sigmoid(mn))
    h2 = mxq(f64(w1), 0, "e4m3").T @ mxq(z, 0, "e4m3")
    mb = h2[:, unstriped(n2)]
    ms = mb.reshape(N, V, 4).sum(axis=2)
    return h2 * sigmoid(ms)

@@ -1,0 +1,238 @@
+from contextlib import ExitStack
+
+import concourse.mybir as mybir
+
+FLOPS = 402653184
+
+F32 = mybir.dt.float32
+BF16 = mybir.dt.bfloat16
+I32 = mybir.dt.int32
+U32 = mybir.dt.uint32
+U16 = mybir.dt.uint16
+U8 = mybir.dt.uint8
+FP8X4 = mybir.dt.float8_e4m3fn_x4
+ALU = mybir.AluOpType
+ACT = mybir.ActivationFunctionType
+
+P = 128
+T = 2048
+S = 512
+V = 256
+W = 1024
+H_SCALE = 0.0625
+
+
+def tile_picked_pqlayhpgategsumg_none_p_kernel(
+    tc, x_words, x_scales, d_words, d_scales, gn, w1, offs, k1, n1, n2, out
+):
+    nc = tc.nc
+    with ExitStack() as ctx:
+        lists = ctx.enter_context(tc.tile_pool(name="lists", bufs=1))
+        keep = ctx.enter_context(tc.tile_pool(name="keep", bufs=1))
+        ring = ctx.enter_context(tc.tile_pool(name="ring", bufs=3))
+        psum = ctx.enter_context(tc.psum_pool(name="psum", bufs=1))
+
+        k1_t = lists.tile([P, S // 16], U16, name="k1_t")
+        offs_t = lists.tile([P, S // 16], U16, name="offs_t")
+        n1_t = lists.tile([P, S // 16], U16, name="n1_t")
+        n2_t = lists.tile([P, W // 16], U16, name="n2_t")
+
+        ds_win = keep.tile([P, T], U8, name="ds_win", align_bytes=64)
+        xs_win = keep.tile([P, T], U8, name="xs_win", align_bytes=64)
+        dw_win = keep.tile([P, T], U32, name="dw_win", tag="early", align_bytes=64)
+        xw_win = keep.tile([P, T], U32, name="xw_win", align_bytes=64)
+
+        def block_rows(scales):
+            return scales[0].bitcast(I32).unsqueeze(1).to_broadcast([16, 8, T // 4])
+
+        nc.sync.dma_start(k1_t[:], k1)
+        nc.sync.dma_start(ds_win[:].bitcast(I32), block_rows(d_scales))
+        nc.sync.dma_start(offs_t[:], offs)
+        nc.sync.dma_start(xs_win[:].bitcast(I32), block_rows(x_scales))
+        nc.sync.dma_start(dw_win[:].bitcast(I32), d_words[0].rearrange("p n t -> p (n t)").bitcast(I32))
+        nc.sync.dma_start(xw_win[:].bitcast(I32), x_words[0].rearrange("p n t -> p (n t)").bitcast(I32))
+        nc.sync.dma_start(n1_t[:], n1)
+        nc.sync.dma_start(n2_t[:], n2)
+        gn_t = keep.tile([P, 4], F32, name="gn_t")
+        nc.scalar.dma_start(gn_t[:], gn.rearrange("(p t) o -> p (t o)", t=4))
+
+        ds_got = keep.tile([P, S], U8, name="ds_got", align_bytes=64)
+        xs_got = keep.tile([P, S], U8, name="xs_got", align_bytes=64)
+        rows = keep.tile([P, 2, S], U8, name="rows", align_bytes=64)
+        nc.vector.tensor_copy(ds_got[:], ds_win[:].indirect(k1_t[:]))
+        nc.vector.tensor_copy(xs_got[:], xs_win[:].indirect(offs_t[:]))
+        nc.vector.tensor_copy(
+            rows[:, 0, :].rearrange("p (t c i) -> p c t i", t=4, i=4),
+            ds_got[:].rearrange("p (c i t) -> p c t i", t=4, i=4),
+        )
+        nc.vector.tensor_copy(rows[:, 1, :].bitcast(I32), xs_got[:].bitcast(I32))
+        rows32 = rows[:].rearrange("p s c -> p (s c)").bitcast(I32)
+        planes = rows
+        planes32 = rows32
+        for a in range(1, 4):
+            nc.scalar.dma_start(planes32[a:P:32, :], rows32[8 * a : P : 32, :])
+
+        dw_got = keep.tile([P, S], U32, name="dw_got", align_bytes=64)
+        dw_dealt = keep.tile([P, S], U32, name="dw_dealt", align_bytes=64)
+        nc.vector.tensor_copy(dw_got[:], dw_win[:].indirect(k1_t[:]))
+        nc.vector.tensor_copy(
+            dw_dealt[:].rearrange("p (t c i) -> p c t i", t=4, i=4),
+            dw_got[:].rearrange("p (c i t) -> p c t i", t=4, i=4),
+        )
+        w_raw = keep.tile([P, 4, S], F32, name="w_raw", tag="early", align_bytes=64)
+        nc.sync.dma_start(w_raw[:], w1.rearrange("(p t) n -> p t n", t=4))
+
+        xw_got = keep.tile([P, S], U32, name="xw_got", align_bytes=64)
+        for half in range(2):
+            nc.vector.tensor_copy(
+                xw_got[:, 256 * half : 256 * (half + 1)], xw_win[:].indirect(offs_t[:, 16 * half : 16 * (half + 1)])
+            )
+
+        h = [keep.tile([P, S], F32, name="h%d" % t, tag="h%d" % t, align_bytes=64) for t in range(4)]
+        ln = keep.tile([P, 4, S], F32, name="ln")
+        mx = keep.tile([P, 4, V], F32, name="mx")
+        mn = keep.tile([P, 4, V], F32, name="mn")
+        sg = keep.tile([P, 4, V], F32, name="sg")
+        z = keep.tile([P, 4, V], F32, name="z")
+        z_bf = keep.tile([P, V, 4], BF16, name="z_bf", align_bytes=64)
+        z_codes = keep.tile([P, V], U32, name="z_codes", align_bytes=64)
+        z_scales = keep.tile([P, V], U8, name="z_scales", align_bytes=64)
+        w_codes = keep.tile([P, S], U32, name="w_codes", align_bytes=64)
+        w_scales = keep.tile([P, S], U8, name="w_scales", align_bytes=64)
+
+        def first_product(on_scalar, t, half):
+            cols = slice(P * t, P * (t + 1))
+            tokens = slice(256 * half, 256 * (half + 1))
+            acc = psum.tile([P, 256], F32, name="acc", tag="bank%d" % (2 * t + half))
+            nc.tensor.matmul_mx(
+                acc[:],
+                lhsT=dw_dealt[:, cols].bitcast(FP8X4),
+                lhsT_scale=planes[:, 0, cols],
+                rhs=xw_got[:, tokens].bitcast(FP8X4),
+                rhs_scale=planes[:, 1, tokens],
+                start=True,
+                stop=True,
+            )
+            if on_scalar:
+                nc.scalar.activation(h[t][:, tokens], acc[:], ACT.Copy, scale=H_SCALE)
+            else:
+                nc.vector.tensor_scalar(h[t][:, tokens], acc[:], H_SCALE, None, ALU.mult)
+
+        def line_up(on_scalar, t, e0, e1):
+            dst = ln[:, t, e0:e1]
+            src = h[t][:].indirect(n1_t[:, e0 // 16 : e1 // 16])
+            if on_scalar:
+                nc.scalar.activation(dst, src, ACT.Copy)
+            else:
+                nc.vector.tensor_copy(dst, src)
+
+        def pairs(t0, t1, v0, v1):
+            both = ln[:, t0:t1, 2 * v0 : 2 * v1].rearrange("p t (v e) -> p t v e", e=2)
+            nc.vector.tensor_tensor(mn[:, t0:t1, v0:v1], both[:, :, :, 0], both[:, :, :, 1], ALU.min)
+            nc.vector.tensor_tensor(mx[:, t0:t1, v0:v1], both[:, :, :, 0], both[:, :, :, 1], ALU.max)
+            nc.scalar.activation(sg[:, t0:t1, v0:v1], mn[:, t0:t1, v0:v1], ACT.Sigmoid)
+
+        def gate(t, v0, v1):
+            nc.vector.scalar_tensor_tensor(
+                z[:, t, v0:v1], mx[:, t, v0:v1], gn_t[:, t : t + 1], sg[:, t, v0:v1], ALU.mult, ALU.mult
+            )
+
+        def weave(copy, dst, src, c0, c1):
+            copy(
+                dst[:, c0:c1, :].rearrange("p (c i) t -> p c t i", i=4),
+                src[:, :, c0:c1].rearrange("p t (c i) -> p c t i", i=4),
+            )
+
+        def quantise(codes, scales, woven, c0, c1):
+            nc.vector.quantize_mx(
+                codes[:, c0:c1].bitcast(FP8X4), scales[:, c0:c1], woven[:, c0:c1, :].rearrange("p c t -> p (c t)")
+            )
+
+        first_product(True, 1, 0)
+        first_product(True, 0, 0)
+        first_product(False, 1, 1)
+        first_product(True, 0, 1)
+        line_up(False, 1, 0, 256)
+        first_product(True, 3, 0)
+        first_product(False, 3, 1)
+        line_up(False, 1, 256, 512)
+        first_product(True, 2, 0)
+        first_product(True, 2, 1)
+        line_up(True, 0, 0, 256)
+        line_up(True, 0, 256, 512)
+        line_up(False, 3, 0, 256)
+        line_up(False, 3, 256, 512)
+        line_up(True, 2, 0, 256)
+        line_up(True, 2, 256, 512)
+        pairs(1, 2, 0, V)
+        pairs(3, 4, 0, V)
+        pairs(0, 1, 0, V)
+        pairs(2, 3, 0, P)
+        pairs(2, 3, P, V)
+        gate(1, 0, V)
+        gate(3, 0, V)
+        gate(0, 0, V)
+        gate(2, 0, V)
+        for half in range(2):
+            weave(nc.vector.tensor_copy, z_bf, z, P * half, P * (half + 1))
+        for half in range(2):
+            quantise(z_codes, z_scales, z_bf, P * half, P * (half + 1))
+        w_bf = keep.tile([P, S, 4], BF16, name="w_bf", tag="h2", align_bytes=64)
+        for m in range(4):
+            weave(nc.scalar.copy, w_bf, w_raw, P * m, P * (m + 1))
+            quantise(w_codes, w_scales, w_bf, P * m, P * (m + 1))
+
+        h2 = []
+        h2_ps = []
+        mb = []
+        res = keep.tile([P, 4, V], F32, name="res")
+
+        def second_product(m):
+            cols = slice(P * m, P * (m + 1))
+            acc = psum.tile([P, V], F32, name="acc", tag="bank%d" % m)
+            nc.tensor.matmul_mx(
+                acc[:],
+                lhsT=w_codes[:, cols].bitcast(FP8X4),
+                lhsT_scale=w_scales[:, cols],
+                rhs=z_codes[:].bitcast(FP8X4),
+                rhs_scale=z_scales[:],
+                start=True,
+                stop=True,
+            )
+            h2_ps.append(acc)
+            h2.append(keep.tile([P, V], F32, name="h2_%d" % m))
+            if m == 0:
+                nc.vector.tensor_copy(h2[m][:], acc[:])
+            else:
+                nc.scalar.copy(h2[m][:], acc[:])
+
+        def members(m, on_vector):
+            mb.append(ring.tile([P, W], F32, name="mb"))
+            for s in range(8):
+                dst = mb[m][:, P * s : P * (s + 1)]
+                src = h2[m][:].indirect(n2_t[:, 8 * s : 8 * (s + 1)])
+                if s < on_vector:
+                    nc.vector.tensor_copy(dst, src)
+                else:
+                    nc.scalar.activation(dst, src, ACT.Copy)
+
+        def finish(add, m, v0, v1):
+            n = v1 - v0
+            two = ring.tile([P, 2 * n], F32, name="two")
+            ms = ring.tile([P, n], F32, name="ms")
+            four = mb[m][:, 4 * v0 : 4 * v1].rearrange("p (u e) -> p u e", e=2)
+            add(two[:], four[:, :, 0], four[:, :, 1], ALU.add)
+            halves = two[:].rearrange("p (u e) -> p u e", e=2)
+            add(ms[:], halves[:, :, 0], halves[:, :, 1], ALU.add)
+            sm = mb[m][:, 4 * v0 : 4 * v0 + n]
+            nc.scalar.activation(sm, ms[:], ACT.Sigmoid)
+            nc.vector.tensor_tensor(res[:, m, v0:v1], h2[m][:, v0:v1], sm, ALU.mult)
+            nc.sync.dma_start(out[P * m : P * (m + 1), v0:v1], res[:, m, v0:v1])
+
+        for m in range(4):
+            second_product(m)
+            members(m, 4)
+            if m > 0:
+                finish(nc.vector.tensor_tensor, m - 1, 0, V)
+        finish(nc.vector.tensor_tensor, 3, 0, P)
+        finish(nc.vector.tensor_tensor, 3, P, V)

@@ -20,6 +20,9 @@ S = 512
 V = 256
 W = 1024
 H_SCALE = 0.0625
+WINDOW = 704
+LAST_CUT = 192
+ON_VECTOR = (512, 416, 384, 352)
 
 
 def tile_picked_pqlayhpgategsumg_none_p_kernel(
@@ -29,13 +32,17 @@ def tile_picked_pqlayhpgategsumg_none_p_kernel(
     with ExitStack() as ctx:
         lists = ctx.enter_context(tc.tile_pool(name="lists", bufs=1))
         keep = ctx.enter_context(tc.tile_pool(name="keep", bufs=1))
-        ring = ctx.enter_context(tc.tile_pool(name="ring", bufs=3))
+        ring = ctx.enter_context(tc.tile_pool(name="ring", bufs=2))
         psum = ctx.enter_context(tc.psum_pool(name="psum", bufs=1))
 
         k1_t = lists.tile([P, S // 16], U16, name="k1_t")
         offs_t = lists.tile([P, S // 16], U16, name="offs_t")
         n1_t = lists.tile([P, S // 16], U16, name="n1_t")
         n2_t = lists.tile([P, W // 16], U16, name="n2_t")
+
+        h = [keep.tile([P, WINDOW], F32, name="h%d" % t) for t in range(4)]
+        for t in range(4):
+            nc.gpsimd.memset(h[t][:, S:], 0.0)
 
         ds_win = keep.tile([P, T], U8, name="ds_win", align_bytes=64)
         xs_win = keep.tile([P, T], U8, name="xs_win", align_bytes=64)
@@ -55,6 +62,9 @@ def tile_picked_pqlayhpgategsumg_none_p_kernel(
         nc.sync.dma_start(n2_t[:], n2)
         gn_t = keep.tile([P, 4], F32, name="gn_t")
         nc.scalar.dma_start(gn_t[:], gn.rearrange("(p t) o -> p (t o)", t=4))
+
+        warm = keep.tile([P, 1], F32, name="warm")
+        nc.scalar.activation(warm[:], gn_t[:, 0:1], ACT.Sigmoid)
 
         ds_got = keep.tile([P, S], U8, name="ds_got", align_bytes=64)
         xs_got = keep.tile([P, S], U8, name="xs_got", align_bytes=64)
@@ -88,10 +98,9 @@ def tile_picked_pqlayhpgategsumg_none_p_kernel(
                 xw_got[:, 256 * half : 256 * (half + 1)], xw_win[:].indirect(offs_t[:, 16 * half : 16 * (half + 1)])
             )
 
-        h = [keep.tile([P, S], F32, name="h%d" % t, tag="h%d" % t, align_bytes=64) for t in range(4)]
         ln = keep.tile([P, 4, S], F32, name="ln")
         mx = keep.tile([P, 4, V], F32, name="mx")
-        mn = keep.tile([P, 4, V], F32, name="mn")
+        mn = keep.tile([P, 4, V], F32, name="mn", tag="mn", align_bytes=64)
         sg = keep.tile([P, 4, V], F32, name="sg")
         z = keep.tile([P, 4, V], F32, name="z")
         z_bf = keep.tile([P, V, 4], BF16, name="z_bf", align_bytes=64)
@@ -100,10 +109,10 @@ def tile_picked_pqlayhpgategsumg_none_p_kernel(
         w_codes = keep.tile([P, S], U32, name="w_codes", align_bytes=64)
         w_scales = keep.tile([P, S], U8, name="w_scales", align_bytes=64)
 
-        def first_product(on_scalar, t, half):
+        def first_product(on_scalar, t, j0, j1):
             cols = slice(P * t, P * (t + 1))
-            tokens = slice(256 * half, 256 * (half + 1))
-            acc = psum.tile([P, 256], F32, name="acc", tag="bank%d" % (2 * t + half))
+            tokens = slice(j0, j1)
+            acc = psum.tile([P, j1 - j0], F32, name="acc", tag="bank%d" % (2 * t + j0 // 256))
             nc.tensor.matmul_mx(
                 acc[:],
                 lhsT=dw_dealt[:, cols].bitcast(FP8X4),
@@ -148,48 +157,37 @@ def tile_picked_pqlayhpgategsumg_none_p_kernel(
                 codes[:, c0:c1].bitcast(FP8X4), scales[:, c0:c1], woven[:, c0:c1, :].rearrange("p c t -> p (c t)")
             )
 
-        first_product(True, 1, 0)
-        first_product(True, 0, 0)
-        first_product(False, 1, 1)
-        first_product(True, 0, 1)
-        line_up(False, 1, 0, 256)
-        first_product(True, 3, 0)
-        first_product(False, 3, 1)
-        line_up(False, 1, 256, 512)
-        first_product(True, 2, 0)
-        first_product(True, 2, 1)
-        line_up(True, 0, 0, 256)
-        line_up(True, 0, 256, 512)
-        line_up(False, 3, 0, 256)
-        line_up(False, 3, 256, 512)
-        line_up(True, 2, 0, 256)
-        line_up(True, 2, 256, 512)
-        pairs(1, 2, 0, V)
+        first_product(True, 0, 0, 256)
+        first_product(True, 2, 0, 256)
+        first_product(False, 0, 256, S)
+        first_product(True, 2, 256, S)
+        line_up(False, 0, 0, S)
+        first_product(True, 1, 0, S)
+        line_up(True, 2, 0, S)
+        line_up(False, 1, 0, S)
+        first_product(True, 3, 0, S)
+        line_up(True, 3, 0, S)
+        pairs(0, 2, 0, V)
+        pairs(2, 3, 0, V)
         pairs(3, 4, 0, V)
-        pairs(0, 1, 0, V)
-        pairs(2, 3, 0, P)
-        pairs(2, 3, P, V)
-        gate(1, 0, V)
-        gate(3, 0, V)
-        gate(0, 0, V)
-        gate(2, 0, V)
-        for half in range(2):
-            weave(nc.vector.tensor_copy, z_bf, z, P * half, P * (half + 1))
-        for half in range(2):
-            quantise(z_codes, z_scales, z_bf, P * half, P * (half + 1))
-        w_bf = keep.tile([P, S, 4], BF16, name="w_bf", tag="h2", align_bytes=64)
+        for t in range(4):
+            gate(t, 0, V)
+        weave(nc.vector.tensor_copy, z_bf, z, 0, V)
+        quantise(z_codes, z_scales, z_bf, 0, V)
+        w_bf = keep.tile([P, S, 4], BF16, name="w_bf", tag="mn", align_bytes=64)
         for m in range(4):
             weave(nc.scalar.copy, w_bf, w_raw, P * m, P * (m + 1))
             quantise(w_codes, w_scales, w_bf, P * m, P * (m + 1))
 
-        h2 = []
         h2_ps = []
         mb = []
+        ms = []
+        sm = keep.tile([P, 4, V], F32, name="sm")
         res = keep.tile([P, 4, V], F32, name="res")
 
         def second_product(m):
             cols = slice(P * m, P * (m + 1))
-            acc = psum.tile([P, V], F32, name="acc", tag="bank%d" % m)
+            acc = psum.tile([P, V], F32, name="acc", tag="bank%d" % (2 * m + 1))
             nc.tensor.matmul_mx(
                 acc[:],
                 lhsT=w_codes[:, cols].bitcast(FP8X4),
@@ -200,39 +198,46 @@ def tile_picked_pqlayhpgategsumg_none_p_kernel(
                 stop=True,
             )
             h2_ps.append(acc)
-            h2.append(keep.tile([P, V], F32, name="h2_%d" % m))
-            if m == 0:
-                nc.vector.tensor_copy(h2[m][:], acc[:])
-            else:
-                nc.scalar.copy(h2[m][:], acc[:])
+            nc.scalar.copy(h[m][:, :V], acc[:])
 
-        def members(m, on_vector):
+        def members(m):
+            split = ON_VECTOR[m]
             mb.append(ring.tile([P, W], F32, name="mb"))
-            for s in range(8):
-                dst = mb[m][:, P * s : P * (s + 1)]
-                src = h2[m][:].indirect(n2_t[:, 8 * s : 8 * (s + 1)])
-                if s < on_vector:
-                    nc.vector.tensor_copy(dst, src)
-                else:
-                    nc.scalar.activation(dst, src, ACT.Copy)
+            nc.vector.tensor_copy(mb[m][:, :split], h[m][:].indirect(n2_t[:, : split // 16]))
+            cuts = [split, W] if m < 3 else [split, 4 * LAST_CUT, W]
+            for e0, e1 in zip(cuts, cuts[1:]):
+                nc.scalar.activation(mb[m][:, e0:e1], h[m][:].indirect(n2_t[:, e0 // 16 : e1 // 16]), ACT.Copy)
 
-        def finish(add, m, v0, v1):
-            n = v1 - v0
-            two = ring.tile([P, 2 * n], F32, name="two")
-            ms = ring.tile([P, n], F32, name="ms")
-            four = mb[m][:, 4 * v0 : 4 * v1].rearrange("p (u e) -> p u e", e=2)
-            add(two[:], four[:, :, 0], four[:, :, 1], ALU.add)
-            halves = two[:].rearrange("p (u e) -> p u e", e=2)
-            add(ms[:], halves[:, :, 0], halves[:, :, 1], ALU.add)
-            sm = mb[m][:, 4 * v0 : 4 * v0 + n]
-            nc.scalar.activation(sm, ms[:], ACT.Sigmoid)
-            nc.vector.tensor_tensor(res[:, m, v0:v1], h2[m][:, v0:v1], sm, ALU.mult)
+        def add_neighbours(add, dst, src):
+            both = src.rearrange("p (u e) -> p u e", e=2)
+            add(dst, both[:, :, 0], both[:, :, 1], ALU.add)
+
+        def sums(add, m, parts):
+            two = ring.tile([P, W // 2], F32, name="two")
+            ms.append(mb[m] if m < 3 else keep.tile([P, V], F32, name="last_sums"))
+            for v0, v1 in parts:
+                add_neighbours(add, two[:, 2 * v0 : 2 * v1], mb[m][:, 4 * v0 : 4 * v1])
+                add_neighbours(add, ms[m][:, v0:v1], two[:, 2 * v0 : 2 * v1])
+
+        def squash(m, v0, v1):
+            nc.scalar.activation(sm[:, m, v0:v1], ms[m][:, v0:v1], ACT.Sigmoid)
+
+        def finish(m, v0, v1):
+            nc.vector.tensor_tensor(res[:, m, v0:v1], h2_ps[m][:, v0:v1], sm[:, m, v0:v1], ALU.mult)
             nc.sync.dma_start(out[P * m : P * (m + 1), v0:v1], res[:, m, v0:v1])
 
         for m in range(4):
             second_product(m)
-            members(m, 4)
             if m > 0:
-                finish(nc.vector.tensor_tensor, m - 1, 0, V)
-        finish(nc.vector.tensor_tensor, 3, 0, P)
-        finish(nc.vector.tensor_tensor, 3, P, V)
+                sums(nc.vector.tensor_tensor, m - 1, [(0, V)])
+            if m > 1:
+                finish(m - 2, 0, V)
+            members(m)
+            if m > 0:
+                squash(m - 1, 0, V)
+        last = ((0, LAST_CUT), (LAST_CUT, V))
+        finish(2, 0, V)
+        sums(nc.vector.tensor_tensor, 3, last)
+        for v0, v1 in last:
+            squash(3, v0, v1)
+            finish(3, v0, v1)

from contextlib import ExitStack

import concourse.mybir as mybir

FLOPS = 402653184

F32 = mybir.dt.float32
BF16 = mybir.dt.bfloat16
I32 = mybir.dt.int32
U32 = mybir.dt.uint32
U16 = mybir.dt.uint16
U8 = mybir.dt.uint8
FP8X4 = mybir.dt.float8_e4m3fn_x4
ALU = mybir.AluOpType
ACT = mybir.ActivationFunctionType

P = 128
T = 2048
S = 512
V = 256
W = 1024
H_SCALE = 0.0625
WINDOW = 704
LAST_CUT = 192
ON_VECTOR = (512, 416, 384, 352)


def tile_picked_pqlayhpgategsumg_none_p_kernel(
    tc, x_words, x_scales, d_words, d_scales, gn, w1, offs, k1, n1, n2, out
):
    nc = tc.nc
    with ExitStack() as ctx:
        lists = ctx.enter_context(tc.tile_pool(name="lists", bufs=1))
        keep = ctx.enter_context(tc.tile_pool(name="keep", bufs=1))
        ring = ctx.enter_context(tc.tile_pool(name="ring", bufs=2))
        psum = ctx.enter_context(tc.psum_pool(name="psum", bufs=1))

        k1_t = lists.tile([P, S // 16], U16, name="k1_t")
        offs_t = lists.tile([P, S // 16], U16, name="offs_t")
        n1_t = lists.tile([P, S // 16], U16, name="n1_t")
        n2_t = lists.tile([P, W // 16], U16, name="n2_t")

        h = [keep.tile([P, WINDOW], F32, name="h%d" % t) for t in range(4)]
        for t in range(4):
            nc.gpsimd.memset(h[t][:, S:], 0.0)

        ds_win = keep.tile([P, T], U8, name="ds_win", align_bytes=64)
        xs_win = keep.tile([P, T], U8, name="xs_win", align_bytes=64)
        dw_win = keep.tile([P, T], U32, name="dw_win", tag="early", align_bytes=64)
        xw_win = keep.tile([P, T], U32, name="xw_win", align_bytes=64)

        def block_rows(scales):
            return scales[0].bitcast(I32).unsqueeze(1).to_broadcast([16, 8, T // 4])

        nc.sync.dma_start(k1_t[:], k1)
        nc.sync.dma_start(ds_win[:].bitcast(I32), block_rows(d_scales))
        nc.sync.dma_start(offs_t[:], offs)
        nc.sync.dma_start(xs_win[:].bitcast(I32), block_rows(x_scales))
        nc.sync.dma_start(dw_win[:].bitcast(I32), d_words[0].rearrange("p n t -> p (n t)").bitcast(I32))
        nc.sync.dma_start(xw_win[:].bitcast(I32), x_words[0].rearrange("p n t -> p (n t)").bitcast(I32))
        nc.sync.dma_start(n1_t[:], n1)
        nc.sync.dma_start(n2_t[:], n2)
        gn_t = keep.tile([P, 4], F32, name="gn_t")
        nc.scalar.dma_start(gn_t[:], gn.rearrange("(p t) o -> p (t o)", t=4))

        warm = keep.tile([P, 1], F32, name="warm")
        nc.scalar.activation(warm[:], gn_t[:, 0:1], ACT.Sigmoid)

        ds_got = keep.tile([P, S], U8, name="ds_got", align_bytes=64)
        xs_got = keep.tile([P, S], U8, name="xs_got", align_bytes=64)
        rows = keep.tile([P, 2, S], U8, name="rows", align_bytes=64)
        nc.vector.tensor_copy(ds_got[:], ds_win[:].indirect(k1_t[:]))
        nc.vector.tensor_copy(xs_got[:], xs_win[:].indirect(offs_t[:]))
        nc.vector.tensor_copy(
            rows[:, 0, :].rearrange("p (t c i) -> p c t i", t=4, i=4),
            ds_got[:].rearrange("p (c i t) -> p c t i", t=4, i=4),
        )
        nc.vector.tensor_copy(rows[:, 1, :].bitcast(I32), xs_got[:].bitcast(I32))
        rows32 = rows[:].rearrange("p s c -> p (s c)").bitcast(I32)
        planes = rows
        planes32 = rows32
        for a in range(1, 4):
            nc.scalar.dma_start(planes32[a:P:32, :], rows32[8 * a : P : 32, :])

        dw_got = keep.tile([P, S], U32, name="dw_got", align_bytes=64)
        dw_dealt = keep.tile([P, S], U32, name="dw_dealt", align_bytes=64)
        nc.vector.tensor_copy(dw_got[:], dw_win[:].indirect(k1_t[:]))
        nc.vector.tensor_copy(
            dw_dealt[:].rearrange("p (t c i) -> p c t i", t=4, i=4),
            dw_got[:].rearrange("p (c i t) -> p c t i", t=4, i=4),
        )
        w_raw = keep.tile([P, 4, S], F32, name="w_raw", tag="early", align_bytes=64)
        nc.sync.dma_start(w_raw[:], w1.rearrange("(p t) n -> p t n", t=4))

        xw_got = keep.tile([P, S], U32, name="xw_got", align_bytes=64)
        for half in range(2):
            nc.vector.tensor_copy(
                xw_got[:, 256 * half : 256 * (half + 1)], xw_win[:].indirect(offs_t[:, 16 * half : 16 * (half + 1)])
            )

        ln = keep.tile([P, 4, S], F32, name="ln")
        mx = keep.tile([P, 4, V], F32, name="mx")
        mn = keep.tile([P, 4, V], F32, name="mn", tag="mn", align_bytes=64)
        sg = keep.tile([P, 4, V], F32, name="sg")
        z = keep.tile([P, 4, V], F32, name="z")
        z_bf = keep.tile([P, V, 4], BF16, name="z_bf", align_bytes=64)
        z_codes = keep.tile([P, V], U32, name="z_codes", align_bytes=64)
        z_scales = keep.tile([P, V], U8, name="z_scales", align_bytes=64)
        w_codes = keep.tile([P, S], U32, name="w_codes", align_bytes=64)
        w_scales = keep.tile([P, S], U8, name="w_scales", align_bytes=64)

        def first_product(on_scalar, t, j0, j1):
            cols = slice(P * t, P * (t + 1))
            tokens = slice(j0, j1)
            acc = psum.tile([P, j1 - j0], F32, name="acc", tag="bank%d" % (2 * t + j0 // 256))
            nc.tensor.matmul_mx(
                acc[:],
                lhsT=dw_dealt[:, cols].bitcast(FP8X4),
                lhsT_scale=planes[:, 0, cols],
                rhs=xw_got[:, tokens].bitcast(FP8X4),
                rhs_scale=planes[:, 1, tokens],
                start=True,
                stop=True,
            )
            if on_scalar:
                nc.scalar.activation(h[t][:, tokens], acc[:], ACT.Copy, scale=H_SCALE)
            else:
                nc.vector.tensor_scalar(h[t][:, tokens], acc[:], H_SCALE, None, ALU.mult)

        def line_up(on_scalar, t, e0, e1):
            dst = ln[:, t, e0:e1]
            src = h[t][:].indirect(n1_t[:, e0 // 16 : e1 // 16])
            if on_scalar:
                nc.scalar.activation(dst, src, ACT.Copy)
            else:
                nc.vector.tensor_copy(dst, src)

        def pairs(t0, t1, v0, v1):
            both = ln[:, t0:t1, 2 * v0 : 2 * v1].rearrange("p t (v e) -> p t v e", e=2)
            nc.vector.tensor_tensor(mn[:, t0:t1, v0:v1], both[:, :, :, 0], both[:, :, :, 1], ALU.min)
            nc.vector.tensor_tensor(mx[:, t0:t1, v0:v1], both[:, :, :, 0], both[:, :, :, 1], ALU.max)
            nc.scalar.activation(sg[:, t0:t1, v0:v1], mn[:, t0:t1, v0:v1], ACT.Sigmoid)

        def gate(t, v0, v1):
            nc.vector.scalar_tensor_tensor(
                z[:, t, v0:v1], mx[:, t, v0:v1], gn_t[:, t : t + 1], sg[:, t, v0:v1], ALU.mult, ALU.mult
            )

        def weave(copy, dst, src, c0, c1):
            copy(
                dst[:, c0:c1, :].rearrange("p (c i) t -> p c t i", i=4),
                src[:, :, c0:c1].rearrange("p t (c i) -> p c t i", i=4),
            )

        def quantise(codes, scales, woven, c0, c1):
            nc.vector.quantize_mx(
                codes[:, c0:c1].bitcast(FP8X4), scales[:, c0:c1], woven[:, c0:c1, :].rearrange("p c t -> p (c t)")
            )

        first_product(True, 0, 0, 256)
        first_product(True, 2, 0, 256)
        first_product(False, 0, 256, S)
        first_product(True, 2, 256, S)
        line_up(False, 0, 0, S)
        first_product(True, 1, 0, S)
        line_up(True, 2, 0, S)
        line_up(False, 1, 0, S)
        first_product(True, 3, 0, S)
        line_up(True, 3, 0, S)
        pairs(0, 2, 0, V)
        pairs(2, 3, 0, V)
        pairs(3, 4, 0, V)
        for t in range(4):
            gate(t, 0, V)
        weave(nc.vector.tensor_copy, z_bf, z, 0, V)
        quantise(z_codes, z_scales, z_bf, 0, V)
        w_bf = keep.tile([P, S, 4], BF16, name="w_bf", tag="mn", align_bytes=64)
        for m in range(4):
            weave(nc.scalar.copy, w_bf, w_raw, P * m, P * (m + 1))
            quantise(w_codes, w_scales, w_bf, P * m, P * (m + 1))

        h2_ps = []
        mb = []
        ms = []
        sm = keep.tile([P, 4, V], F32, name="sm")
        res = keep.tile([P, 4, V], F32, name="res")

        def second_product(m):
            cols = slice(P * m, P * (m + 1))
            acc = psum.tile([P, V], F32, name="acc", tag="bank%d" % (2 * m + 1))
            nc.tensor.matmul_mx(
                acc[:],
                lhsT=w_codes[:, cols].bitcast(FP8X4),
                lhsT_scale=w_scales[:, cols],
                rhs=z_codes[:].bitcast(FP8X4),
                rhs_scale=z_scales[:],
                start=True,
                stop=True,
            )
            h2_ps.append(acc)
            nc.scalar.copy(h[m][:, :V], acc[:])

        def members(m):
            split = ON_VECTOR[m]
            mb.append(ring.tile([P, W], F32, name="mb"))
            nc.vector.tensor_copy(mb[m][:, :split], h[m][:].indirect(n2_t[:, : split // 16]))
            cuts = [split, W] if m < 3 else [split, 4 * LAST_CUT, W]
            for e0, e1 in zip(cuts, cuts[1:]):
                nc.scalar.activation(mb[m][:, e0:e1], h[m][:].indirect(n2_t[:, e0 // 16 : e1 // 16]), ACT.Copy)

        def add_neighbours(add, dst, src):
            both = src.rearrange("p (u e) -> p u e", e=2)
            add(dst, both[:, :, 0], both[:, :, 1], ALU.add)

        def sums(add, m, parts):
            two = ring.tile([P, W // 2], F32, name="two")
            ms.append(mb[m] if m < 3 else keep.tile([P, V], F32, name="last_sums"))
            for v0, v1 in parts:
                add_neighbours(add, two[:, 2 * v0 : 2 * v1], mb[m][:, 4 * v0 : 4 * v1])
                add_neighbours(add, ms[m][:, v0:v1], two[:, 2 * v0 : 2 * v1])

        def squash(m, v0, v1):
            nc.scalar.activation(sm[:, m, v0:v1], ms[m][:, v0:v1], ACT.Sigmoid)

        def finish(m, v0, v1):
            nc.vector.tensor_tensor(res[:, m, v0:v1], h2_ps[m][:, v0:v1], sm[:, m, v0:v1], ALU.mult)
            nc.sync.dma_start(out[P * m : P * (m + 1), v0:v1], res[:, m, v0:v1])

        for m in range(4):
            second_product(m)
            if m > 0:
                sums(nc.vector.tensor_tensor, m - 1, [(0, V)])
            if m > 1:
                finish(m - 2, 0, V)
            members(m)
            if m > 0:
                squash(m - 1, 0, V)
        last = ((0, LAST_CUT), (LAST_CUT, V))
        finish(2, 0, V)
        sums(nc.vector.tensor_tensor, 3, last)
        for v0, v1 in last:
            squash(3, v0, v1)
            finish(3, v0, v1)
